import numpy as np, ml_dtypes
CORES = [56,61,80,85]
N = 4
J, Q = 512, 2048
def entries(a): return a.T.reshape(-1)
def pack(v, P): return np.ascontiguousarray(np.asarray(v, np.int32).reshape(-1, P).T)
def split(rng, total, parts):
    c = np.sort(rng.integers(0, total + 1, parts - 1)); return np.diff(np.concatenate([[0], c, [total]]))
def lists(rng, how):
    tot = 1 + split(rng, int(rng.integers(N * Q - Q // 2, N * Q + 1)) - N, N)
    if how == "gaps": tot = split(rng, (N - 1) * Q, N)
    if how == "short": tot = split(rng, Q * int(rng.integers(1, N - 1)) + int(rng.integers(1, Q)), N)
    L = np.stack([split(rng, int(t), J) for t in tot])
    if how == "gaps":
        L = np.zeros((N, J), np.int64)
        for r in range(N): m = 1 if r & 1 else 8; L[r, 1 + rng.permutation(J - 2)[:m]] = split(rng, int(tot[r]), m)
    if how == "lone":
        L = np.zeros((N, J), np.int64); L[int(rng.integers(N)), int(rng.integers(J))] = N * Q
    if how == "ones":
        L = np.zeros((N, J), np.int64)
        for r in range(N): L[r, rng.permutation(J)[:min(J, Q // N)]] = 1
    if how == "void": L[:] = 0
    return {"ln": np.stack([pack(l, 16) for l in L])}
def setup_inputs(rng):
    return dict({"x": rng.standard_normal((N, 128, J), dtype=np.float32).astype(ml_dtypes.bfloat16)}, **lists(rng, "uniform"))
def setup_inputs_gaps(rng):
    d = setup_inputs(rng); d.update(lists(rng, "gaps"))
    for k in ("x",): d[k] = (d[k].astype(np.float32) * 1048576.0).astype(d[k].dtype)
    return d
def setup_inputs_lone(rng):
    d = setup_inputs(rng); d.update(lists(rng, "lone"))
    for k in ("x",): d[k] = (d[k].astype(np.float32) * (1 / 1024.0)).astype(d[k].dtype)
    return d
def setup_inputs_ones(rng):
    d = setup_inputs(rng); d.update(lists(rng, "ones"))
    return d
def setup_inputs_short(rng):
    d = setup_inputs(rng); d.update(lists(rng, "short"))
    return d
def setup_inputs_void(rng):
    d = setup_inputs(rng); d.update(lists(rng, "void"))
    return d
def check_inputs(x):
    bad = []
    if x["ln"].min() < 0 or x["ln"].max() >= N * Q + 1: bad.append("ln out of range")
    if int(x["ln"].sum()) > N * Q: bad.append("the lengths come to more than N * Q")
    return bad
def reference(x, ln):
    got = np.concatenate([np.repeat(x[r], entries(ln[r]), axis=1) for r in range(N)], axis=1)[:, :N * Q]
    Y = np.zeros((128, N * Q), x.dtype); Y[:, :got.shape[1]] = got
    return {"y": np.stack([Y[:, Q * r:Q * r + Q] for r in range(N)])}

@@ -1,0 +1,292 @@
+from concourse.bass import DstId, RemoteDMATransfer
+from concourse.mybir import AluOpType as Op, AxisListType, ActivationFunctionType as Act
+
+J, Q = 512, 2048
+NT = 16
+QB = 32
+NC = Q // QB
+SW = 72
+NV = 5
+GROUPS = ((0, 6), (6, 11), (11, 14), (14, 16))
+LW = 20
+STEPS = (384, 384, 256)
+
+SCRATCH = {
+    "win": ("sbuf", [128, 4 * J + 8], "bfloat16"),
+    "lnat": ("sbuf", [128, 32], "int32"),
+    "lraw": ("sbuf", [128, 32], "int32"),
+    "lsum": ("sbuf", [128, 32], "int32"),
+    "ltr": ("sbuf", [128, 32], "int32"),
+    "lend": ("sbuf", [128, 4 * LW], "float32"),
+    "lchip": ("sbuf", [128, 16], "float32"),
+    "base": ("sbuf", [128, 4], "float32"),
+    "shift": ("sbuf", [128, 16], "float32"),
+    "echip": ("sbuf", [128, 16], "float32"),
+    "ends": ("sbuf", [128, LW], "float32"),
+    "blk": ("sbuf", [128, 16], "int32"),
+    "zblk": ("sbuf", [128, 16], "float32"),
+    "diff": ("sbuf", [128, 128], "bfloat16"),
+    "val": ("sbuf", [128, 128], "bfloat16"),
+    "thr": ("sbuf", [128, SW], "bfloat16"),
+    "qtab": ("sbuf", [128, QB], "bfloat16"),
+    "tri": ("sbuf", [128, 128], "float32"),
+    "pcol": ("sbuf", [32, 4], "float32"),
+    "up0": ("sbuf", [32, 128], "float16"),
+    "up1": ("sbuf", [32, 128], "float16"),
+    "dn0": ("sbuf", [32, 128], "float16"),
+    "dn1": ("sbuf", [32, 128], "float16"),
+    "ah": ("sbuf", [128, NT * QB], "bfloat16"),
+    "sg": ("sbuf", [128, NT * SW], "bfloat16"),
+    "wh": ("sbuf", [32, SW], "float16"),
+    "off": ("sbuf", [128, 128], "uint16"),
+    "yo": ("sbuf", [128, Q], "bfloat16"),
+    "psb": ("psum", [128, 512], "float32"),
+    "psw": ("psum", [128, 512], "float32"),
+    "pso0": ("psum", [128, 512], "float32"),
+    "pso1": ("psum", [128, 512], "float32"),
+}
+SEMAPHORES = (["l0", "l1", "l2", "l3", "x0", "x1", "x2", "x3", "t0", "t1", "tn", "ls", "dl", "dx", "st"]
+              + ["mz", "mw", "ms", "su", "tr", "i_d", "i_t", "c_tri", "c_pc", "c_up", "c_dn", "lo", "pb", "bs",
+                 "ec", "en", "ei", "em", "pw", "wc", "po0", "po1", "of"]
+              + ["a%d" % i for i in range(len(GROUPS))] + ["s%d" % i for i in range(len(GROUPS))]
+              + ["yv%d" % i for i in range(len(STEPS))] + ["ys%d" % i for i in range(len(STEPS))])
+
+
+def _engines(mask):
+    return bin(mask).count("1")
+
+
+def _routes(T, topo, rank):
+    me = T.cores[rank]
+    near = [r for r, c in enumerate(T.cores) if c != me and topo.chip(c) == topo.chip(me)]
+    far = [r for r, c in enumerate(T.cores) if topo.chip(c) != topo.chip(me)]
+    hi = me
+    while topo.chip(hi + 1) == topo.chip(me):
+        hi += 1
+    lo = me
+    while lo > 0 and topo.chip(lo - 1) == topo.chip(me):
+        lo -= 1
+    own = [c for c in range(lo, hi + 1) if T.rank_of(c) is None and topo.die(c) == topo.die(me)
+           and all(topo.may_write(c, T.cores[f]) for f in far)]
+    return near, [(own[i % len(own)], f) for i, f in enumerate(far)]
+
+
+def _dst(topo, c):
+    rid, pid, _ = topo.addr(c)
+    return DstId(rid=rid, pnc=pid)
+
+
+def _lslot(r):
+    return slice(LW * r, LW * r + 17)
+
+
+def _xslot(r):
+    return slice(J * r, J * r + J)
+
+
+def rank_program(g, core, T, topo):
+    rank = T.rank_of(core)
+    if rank is None:
+        _relay(g, core, T, topo)
+    else:
+        _rank(g, core, rank, T, topo)
+
+
+def _relay(g, core, T, topo):
+    s, v, pe = T.sem, g.vector, g.tensor
+    for r in range(len(T.cores)):
+        for i, (relay, f) in enumerate(_routes(T, topo, r)[1]):
+            if relay != core:
+                continue
+            home, dst = T.cores[r], T.cores[f]
+            here = _engines(topo.mask(home, core))
+            m = topo.mask(core, dst)
+            sent = 0
+
+            def send(ap, to, sem):
+                rid, pid, _ = topo.addr(to)
+                em = m & topo.mask(core, to)
+                g.remote_dma(out_ap=ap, in_ap=ap, remote_sem=sem, local_sem=s.ls, pid=pid, routing_id=rid,
+                             dma_engine_mask=em)
+                return _engines(em)
+
+            g.iota(T.diff[:], [[1, 128]], 0, -1, allow_small_or_imprecise_dtypes=True).then_inc(s.i_d, 1)
+            if i == 0:
+                g.wait_ge(s.i_d, 1)
+                sent += send(T.diff[:], home, s.t0)
+            else:
+                g.iota(T.val[:], [[0, 8], [1, 16]], 0, -1, allow_small_or_imprecise_dtypes=True).then_inc(s.i_t, 1)
+                g.wait_ge(s.i_t, 1)
+                sent += send(T.val[:], home, s.t1)
+            v.wait_ge(s.i_d, 1)
+            v.tensor_scalar(T.tri[:], T.diff[:], 0.0, None, Op.is_gt).then_inc(s.c_tri, 1)
+            lens = T.lend[:, LW * r + 1:LW * r + 17]
+            v.wait_ge(s["l%d" % r], here)
+            v.transpose(T.ltr[:], T.lraw[:]).then_inc(s.tr, 1)
+            v.wait_ge(s.tr, 1)
+            v.tensor_scalar(lens, T.ltr[:, 16:32], 2.0, None, Op.mult).then_inc(s.lo, 1)
+            pe.wait_ge(s.c_tri, 1)
+            pe.wait_ge(s.lo, 1)
+            pe.matmul(T.psb[:, 0:16], T.tri[:], lens, True, True).then_inc(s.pb, 1)
+            v.wait_ge(s.pb, 1)
+            v.tensor_reduce(T.lend[:, LW * r:LW * r + 1], T.psb[:, 0:16], AxisListType.X, Op.add).then_inc(s.bs, 1)
+            g.wait_ge(s.lo, 1)
+            g.wait_ge(s.bs, 1)
+            sent += send(T.lend[:, _lslot(r)], dst, s["l%d" % r])
+            g.wait_ge(s["x%d" % r], here)
+            sent += send(T.win[:, _xslot(r)], dst, s["x%d" % r])
+            g.wait_ge(s.ls, sent)
+
+
+def _rank(g, core, r, T, topo):
+    s, v, pe, sc, sy = T.sem, g.vector, g.tensor, g.scalar, g.sync
+    near, relays = _routes(T, topo, r)
+    far = [f for _, f in relays]
+    tinc = [_engines(topo.mask(relay, core) & topo.mask(relay, T.cores[f])) for relay, f in relays]
+    inc = {}
+    for o in near:
+        inc[o] = _engines(topo.mask(T.cores[o], core))
+    for o in far:
+        for relay, f in _routes(T, topo, o)[1]:
+            if f == r:
+                inc[o] = _engines(topo.mask(relay, core))
+
+    sy.dma_start(T.lnat[32 * r + 16:32 * r + 32, :], T.ln[:]).then_inc(s.dl, 16)
+    sc.dma_start(T.win[:, _xslot(r)], T.x[:]).then_inc(s.dx, 16)
+
+    if r < min(near):
+        table = T.thr[:, 0:NC + 1]
+        g.iota(table, [[2 * QB, NC + 1]], -QB, 0, allow_small_or_imprecise_dtypes=True).then_inc(s.i_t, 1)
+    else:
+        table = T.qtab[:]
+        g.iota(table, [[2, QB]], 1 - QB, 0, allow_small_or_imprecise_dtypes=True).then_inc(s.i_t, 1)
+    sent = 0
+
+    def send(src, out, sem, cores):
+        m = topo.mask(core, cores[0])
+        g.remote_dma_fused([RemoteDMATransfer(dst_ids=[_dst(topo, c) for c in cores], dma_engine_mask=m, remote_sem=sem,
+                                              srcs=[src], dsts=[out for _ in cores])], local_sem=s.ls)
+        return _engines(m)
+
+    hop = [c for c, _ in relays]
+    nb = [T.cores[o] for o in near]
+    own = T.win[:, _xslot(r)]
+    g.wait_ge(s.i_t, 1)
+    sent += send(table, table, s.tn, nb)
+    g.wait_ge(s.mz, 4)
+    g.wait_ge(s.dl, 16)
+    sent += send(T.lnat[:], T.lraw[:], s["l%d" % r], hop + nb)
+    g.wait_ge(s.dx, 16)
+    sent += send(own, own, s["x%d" % r], hop)
+    sent += send(own, own, s["x%d" % r], nb)
+
+    for b in range(4):
+        v.memset(T.lnat[32 * b:32 * b + (16 if b == r else 32), :], 0).then_inc(s.mz, 1)
+    v.memset(T.win[:, 4 * J:4 * J + 8], 0.0).then_inc(s.mw, 1)
+    v.memset(T.shift[:, 0:1], float(1 - QB - 2 * Q * r)).then_inc(s.ms, 1)
+    v.memset(T.shift[:, 1:16], 0.0).then_inc(s.ms, 1)
+    v.wait_ge(s.t0, tinc[0])
+    v.tensor_scalar(T.tri[:], T.diff[:], 0.0, None, Op.is_gt).then_inc(s.c_tri, 1)
+    v.wait_ge(s.t1, tinc[1])
+    v.tensor_scalar(T.pcol[:, 0:1], T.val[0:32, 0:1], float(1 - QB), -0.5, Op.is_equal, Op.mult).then_inc(s.c_pc, 1)
+    for h in range(2):
+        v.tensor_scalar(T["up%d" % h][:], T.val[0:32, :], -16.0 * h, -0.5, Op.is_equal, Op.mult).then_inc(s.c_up, 1)
+    v.wait_ge(s.c_pc, 1)
+    v.wait_ge(s.c_up, 2)
+    for h in range(2):
+        v.tensor_scalar(T["dn%d" % h][:], T["up%d" % h][:], -1.0, T.pcol[:, 0:1], Op.mult, Op.add).then_inc(s.c_dn, 1)
+
+    v.wait_ge(s.mz, 4)
+    v.wait_ge(s.dl, 16)
+    v.wait_ge(s["l%d" % near[0]], inc[near[0]])
+    v.tensor_tensor(T.lsum[:], T.lnat[:], T.lraw[:], Op.add).then_inc(s.su, 1)
+    v.wait_ge(s.su, 1)
+    v.transpose(T.ltr[:], T.lsum[:]).then_inc(s.tr, 1)
+    v.wait_ge(s.tr, 1)
+    v.tensor_scalar(T.lchip[:], T.ltr[:, 16:32], 2.0, None, Op.mult).then_inc(s.lo, 1)
+    pe.wait_ge(s.c_tri, 1)
+    pe.wait_ge(s.lo, 1)
+    pe.matmul(T.psb[:, 0:16], T.tri[:], T.lchip[:], True, True).then_inc(s.pb, 1)
+    v.wait_ge(s.lo, 1)
+    v.wait_ge(s.ms, 2)
+    v.wait_ge(s.pb, 1)
+    v.tensor_reduce(T.base[:, 0:1], T.psb[:, 0:16], AxisListType.X, Op.add).then_inc(s.bs, 1)
+    v.wait_ge(s.bs, 1)
+    v.tensor_tensor_scan(T.echip[:], T.lchip[:], T.shift[:], T.base[:, 0:1], Op.add, Op.add).then_inc(s.ec, 1)
+
+    v.wait_ge(s.ec, 1)
+    for q in (v, sc):
+        q.wait_ge(s.i_t, 1)
+        q.wait_ge(s.tn, inc[near[0]])
+    for o in far:
+        v.wait_ge(s["l%d" % o], inc[o])
+    there = slice(32 * min(far), 32 * max(far) + 32)
+    here = slice(32 * min(near + [r]), 32 * max(near + [r]) + 32)
+    f0, f1 = LW * far[0], LW * far[1]
+    v.tensor_tensor_scan(T.ends[there, 0:17], T.lend[there, f0:f0 + 17], T.lend[there, f1:f1 + 17], T.echip[there, 0:1],
+                         Op.add, Op.add).then_inc(s.en, 1)
+    v.tensor_scalar(T.ends[here, 1:17], T.echip[here, :], T.lend[here, f0:f0 + 1], T.lend[here, f1:f1 + 1],
+                    Op.add, Op.add).then_inc(s.en, 1)
+    group = [i for i, (t0, t1) in enumerate(GROUPS) for _ in range(t0, t1)]
+    thr = T.thr[:, 0:NC + 1]
+
+    def row(t):
+        return T.sg[:, SW * t:SW * t + NC + 1]
+
+    def end(t):
+        return T.ends[:, t + 1:t + 2]
+
+    sc.wait_ge(s.en, 2)
+    for t in range(NV, NT):
+        sc.activation(row(t), thr, Act.Sign, bias=end(t), scale=-1.0).then_inc(s["s%d" % group[t]], 1)
+    def share(a, b):
+        for t in range(a, b):
+            v.tensor_scalar(row(t), thr, end(t), 2.0, Op.is_lt, Op.mult).then_inc(s["s%d" % group[t]], 1)
+
+    v.wait_ge(s.en, 2)
+    v.tensor_scalar(T.blk[:], T.ends[:, 1:17], 0.5 / QB, None, Op.mult).then_inc(s.ei, 1)
+    share(0, 2)
+    v.wait_ge(s.ei, 1)
+    v.tensor_scalar(T.zblk[:], T.blk[:], 2.0 * QB, None, Op.mult).then_inc(s.em, 1)
+    share(2, NV)
+    v.wait_ge(s.em, 1)
+    for t in range(NT):
+        v.tensor_scalar(T.ah[:, QB * t:QB * t + QB], T.qtab[:], T.zblk[:, t:t + 1], end(t),
+                        Op.add, Op.is_ge).then_inc(s["a%d" % group[t]], 1)
+    for i, (t0, t1) in enumerate(GROUPS):
+        pe.wait_ge(s["a%d" % i], t1 - t0)
+        pe.wait_ge(s["s%d" % i], t1 - t0)
+        for t in range(t0, t1):
+            mm = pe.matmul(T.psw[0:QB, 0:NC + 1], T.ah[:, QB * t:QB * t + QB], row(t), t == 0, t == NT - 1)
+    mm.then_inc(s.pw, 1)
+    v.wait_ge(s.pw, 1)
+    v.tensor_scalar(T.wh[:, 0:NC + 1], T.psw[0:QB, 0:NC + 1], -128.0 * NV, None, Op.add).then_inc(s.wc, 1)
+    pe.wait_ge(s.c_up, 2)
+    pe.wait_ge(s.c_dn, 2)
+    pe.wait_ge(s.wc, 1)
+    for h in range(2):
+        out = T["pso%d" % h][:, 0:NC]
+        pe.matmul(out, T["up%d" % h][:], T.wh[:, 1:NC + 1], True, False)
+        pe.matmul(out, T["dn%d" % h][:], T.wh[:, 0:NC], False, True).then_inc(s["po%d" % h], 1)
+    for h in range(2):
+        v.wait_ge(s["po%d" % h], 1)
+        v.tensor_scalar(T.off[:, h::2], T["pso%d" % h][:, 0:NC], float(Q // 2), None, Op.add).then_inc(s.of, 1)
+
+    for q in (v, sc):
+        q.wait_ge(s.mw, 1)
+        q.wait_ge(s.of, 2)
+        q.wait_ge(s.dx, 16)
+        for o in near + far:
+            q.wait_ge(s["x%d" % o], inc[o])
+    win = T.win[:, 0:4 * J + 8]
+    at = 0
+    for i, w in enumerate(STEPS):
+        mid, stop = at + w, at + 2 * w
+        v.tensor_copy(T.yo[:, at:mid], win.indirect(T.off[:, at // 16:mid // 16])).then_inc(s["yv%d" % i], 1)
+        sc.activation(T.yo[:, mid:stop], win.indirect(T.off[:, mid // 16:stop // 16]), Act.Copy).then_inc(s["ys%d" % i], 1)
+        sy.wait_ge(s["yv%d" % i], 1)
+        sy.wait_ge(s["ys%d" % i], 1)
+        sy.dma_start(T.y[:, at:stop], T.yo[:, at:stop]).then_inc(s.st, 16)
+        at = stop
+    sy.wait_ge(s.st, 16 * len(STEPS))
+    g.wait_ge(s.ls, sent)

@@ -6,7 +6,8 @@ NT = 16
 QB = 32
 NC = Q // QB
 SW = 72
-NV = 5
+NV = 1
+ROUND = 1.5 * 2.0 ** 29
 GROUPS = ((0, 6), (6, 11), (11, 14), (14, 16))
 LW = 20
 STEPS = (384, 384, 256)
@@ -23,7 +24,6 @@ SCRATCH = {
     "shift": ("sbuf", [128, 16], "float32"),
     "echip": ("sbuf", [128, 16], "float32"),
     "ends": ("sbuf", [128, LW], "float32"),
-    "blk": ("sbuf", [128, 16], "int32"),
     "zblk": ("sbuf", [128, 16], "float32"),
     "diff": ("sbuf", [128, 128], "bfloat16"),
     "val": ("sbuf", [128, 128], "bfloat16"),
@@ -47,7 +47,7 @@ SCRATCH = {
 }
 SEMAPHORES = (["l0", "l1", "l2", "l3", "x0", "x1", "x2", "x3", "t0", "t1", "tn", "ls", "dl", "dx", "st"]
               + ["mz", "mw", "ms", "su", "tr", "i_d", "i_t", "c_tri", "c_pc", "c_up", "c_dn", "lo", "pb", "bs",
-                 "ec", "en", "ei", "em", "pw", "wc", "po0", "po1", "of"]
+                 "ec", "en", "em", "pw", "wc", "po0", "po1", "of"]
               + ["a%d" % i for i in range(len(GROUPS))] + ["s%d" % i for i in range(len(GROUPS))]
               + ["yv%d" % i for i in range(len(STEPS))] + ["ys%d" % i for i in range(len(STEPS))])
 
@@ -175,7 +175,8 @@ def _rank(g, core, r, T, topo):
     sent += send(table, table, s.tn, nb)
     g.wait_ge(s.mz, 4)
     g.wait_ge(s.dl, 16)
-    sent += send(T.lnat[:], T.lraw[:], s["l%d" % r], hop + nb)
+    sent += send(T.lnat[:], T.lraw[:], s["l%d" % r], hop)
+    sent += send(T.lnat[:], T.lraw[:], s["l%d" % r], nb)
     g.wait_ge(s.dx, 16)
     sent += send(own, own, s["x%d" % r], hop)
     sent += send(own, own, s["x%d" % r], nb)
@@ -185,21 +186,13 @@ def _rank(g, core, r, T, topo):
     v.memset(T.win[:, 4 * J:4 * J + 8], 0.0).then_inc(s.mw, 1)
     v.memset(T.shift[:, 0:1], float(1 - QB - 2 * Q * r)).then_inc(s.ms, 1)
     v.memset(T.shift[:, 1:16], 0.0).then_inc(s.ms, 1)
-    v.wait_ge(s.t0, tinc[0])
-    v.tensor_scalar(T.tri[:], T.diff[:], 0.0, None, Op.is_gt).then_inc(s.c_tri, 1)
-    v.wait_ge(s.t1, tinc[1])
-    v.tensor_scalar(T.pcol[:, 0:1], T.val[0:32, 0:1], float(1 - QB), -0.5, Op.is_equal, Op.mult).then_inc(s.c_pc, 1)
-    for h in range(2):
-        v.tensor_scalar(T["up%d" % h][:], T.val[0:32, :], -16.0 * h, -0.5, Op.is_equal, Op.mult).then_inc(s.c_up, 1)
-    v.wait_ge(s.c_pc, 1)
-    v.wait_ge(s.c_up, 2)
-    for h in range(2):
-        v.tensor_scalar(T["dn%d" % h][:], T["up%d" % h][:], -1.0, T.pcol[:, 0:1], Op.mult, Op.add).then_inc(s.c_dn, 1)
 
     v.wait_ge(s.mz, 4)
     v.wait_ge(s.dl, 16)
     v.wait_ge(s["l%d" % near[0]], inc[near[0]])
     v.tensor_tensor(T.lsum[:], T.lnat[:], T.lraw[:], Op.add).then_inc(s.su, 1)
+    v.wait_ge(s.t0, tinc[0])
+    v.tensor_scalar(T.tri[:], T.diff[:], 0.0, None, Op.is_gt).then_inc(s.c_tri, 1)
     v.wait_ge(s.su, 1)
     v.transpose(T.ltr[:], T.lsum[:]).then_inc(s.tr, 1)
     v.wait_ge(s.tr, 1)
@@ -213,6 +206,15 @@ def _rank(g, core, r, T, topo):
     v.tensor_reduce(T.base[:, 0:1], T.psb[:, 0:16], AxisListType.X, Op.add).then_inc(s.bs, 1)
     v.wait_ge(s.bs, 1)
     v.tensor_tensor_scan(T.echip[:], T.lchip[:], T.shift[:], T.base[:, 0:1], Op.add, Op.add).then_inc(s.ec, 1)
+
+    v.wait_ge(s.t1, tinc[1])
+    v.tensor_scalar(T.pcol[:, 0:1], T.val[0:32, 0:1], float(1 - QB), -0.5, Op.is_equal, Op.mult).then_inc(s.c_pc, 1)
+    for h in range(2):
+        v.tensor_scalar(T["up%d" % h][:], T.val[0:32, :], -16.0 * h, -0.5, Op.is_equal, Op.mult).then_inc(s.c_up, 1)
+    v.wait_ge(s.c_pc, 1)
+    v.wait_ge(s.c_up, 2)
+    for h in range(2):
+        v.tensor_scalar(T["dn%d" % h][:], T["up%d" % h][:], -1.0, T.pcol[:, 0:1], Op.mult, Op.add).then_inc(s.c_dn, 1)
 
     v.wait_ge(s.ec, 1)
     for q in (v, sc):
@@ -239,16 +241,10 @@ def _rank(g, core, r, T, topo):
     sc.wait_ge(s.en, 2)
     for t in range(NV, NT):
         sc.activation(row(t), thr, Act.Sign, bias=end(t), scale=-1.0).then_inc(s["s%d" % group[t]], 1)
-    def share(a, b):
-        for t in range(a, b):
-            v.tensor_scalar(row(t), thr, end(t), 2.0, Op.is_lt, Op.mult).then_inc(s["s%d" % group[t]], 1)
-
     v.wait_ge(s.en, 2)
-    v.tensor_scalar(T.blk[:], T.ends[:, 1:17], 0.5 / QB, None, Op.mult).then_inc(s.ei, 1)
-    share(0, 2)
-    v.wait_ge(s.ei, 1)
-    v.tensor_scalar(T.zblk[:], T.blk[:], 2.0 * QB, None, Op.mult).then_inc(s.em, 1)
-    share(2, NV)
+    v.tensor_scalar(T.zblk[:], T.ends[:, 1:17], ROUND, -ROUND, Op.add, Op.add).then_inc(s.em, 1)
+    for t in range(NV):
+        v.tensor_scalar(row(t), thr, end(t), 2.0, Op.is_lt, Op.mult).then_inc(s["s%d" % group[t]], 1)
     v.wait_ge(s.em, 1)
     for t in range(NT):
         v.tensor_scalar(T.ah[:, QB * t:QB * t + QB], T.qtab[:], T.zblk[:, t:t + 1], end(t),

@@ -10,26 +10,24 @@ NV = 1
 ROUND = 1.5 * 2.0 ** 29
 GROUPS = ((0, 6), (6, 11), (11, 14), (14, 16))
 LW = 20
-STEPS = (384, 384, 256)
+STEPS = (256, 320, 256, 192)
 
 SCRATCH = {
     "win": ("sbuf", [128, 4 * J + 8], "bfloat16"),
     "lnat": ("sbuf", [128, 32], "int32"),
-    "lraw": ("sbuf", [128, 32], "int32"),
-    "lsum": ("sbuf", [128, 32], "int32"),
     "ltr": ("sbuf", [128, 32], "int32"),
     "lend": ("sbuf", [128, 4 * LW], "float32"),
-    "lchip": ("sbuf", [128, 16], "float32"),
-    "base": ("sbuf", [128, 4], "float32"),
-    "shift": ("sbuf", [128, 16], "float32"),
-    "echip": ("sbuf", [128, 16], "float32"),
+    "shift": ("sbuf", [128, 4], "float32"),
+    "echip": ("sbuf", [128, LW], "float32"),
     "ends": ("sbuf", [128, LW], "float32"),
     "zblk": ("sbuf", [128, 16], "float32"),
-    "diff": ("sbuf", [128, 128], "bfloat16"),
+    "ones": ("sbuf", [128, 32], "float32"),
+    "idx": ("sbuf", [128, 32], "float32"),
+    "idxt": ("sbuf", [128, 32], "float32"),
+    "tri": ("sbuf", [128, 128], "float32"),
     "val": ("sbuf", [128, 128], "bfloat16"),
     "thr": ("sbuf", [128, SW], "bfloat16"),
     "qtab": ("sbuf", [128, QB], "bfloat16"),
-    "tri": ("sbuf", [128, 128], "float32"),
     "pcol": ("sbuf", [32, 4], "float32"),
     "up0": ("sbuf", [32, 128], "float16"),
     "up1": ("sbuf", [32, 128], "float16"),
@@ -46,8 +44,8 @@ SCRATCH = {
     "pso1": ("psum", [128, 512], "float32"),
 }
 SEMAPHORES = (["l0", "l1", "l2", "l3", "x0", "x1", "x2", "x3", "t0", "t1", "tn", "ls", "dl", "dx", "st"]
-              + ["mz", "mw", "ms", "su", "tr", "i_d", "i_t", "c_tri", "c_pc", "c_up", "c_dn", "lo", "pb", "bs",
-                 "ec", "en", "em", "pw", "wc", "po0", "po1", "of"]
+              + ["mz", "me", "mo", "mt", "mw", "ms", "tr", "i_t", "c_ix", "c_it", "c_tri", "c_pc", "c_up", "c_dn", "lo", "pb",
+                 "bs", "ec", "en", "em", "pw", "wc", "po0", "po1", "of"]
               + ["a%d" % i for i in range(len(GROUPS))] + ["s%d" % i for i in range(len(GROUPS))]
               + ["yv%d" % i for i in range(len(STEPS))] + ["ys%d" % i for i in range(len(STEPS))])
 
@@ -93,7 +91,7 @@ def rank_program(g, core, T, topo):
 
 
 def _relay(g, core, T, topo):
-    s, v, pe = T.sem, g.vector, g.tensor
+    s = T.sem
     for r in range(len(T.cores)):
         for i, (relay, f) in enumerate(_routes(T, topo, r)[1]):
             if relay != core:
@@ -101,40 +99,22 @@ def _relay(g, core, T, topo):
             home, dst = T.cores[r], T.cores[f]
             here = _engines(topo.mask(home, core))
             m = topo.mask(core, dst)
+            if i == 0:
+                table = T.thr[:, 0:NC + 1]
+                g.iota(table, [[2 * QB, NC + 1]], -QB, 0, allow_small_or_imprecise_dtypes=True).then_inc(s.i_t, 1)
+            else:
+                table = T.val[:]
+                g.iota(table, [[0, 8], [1, 16]], 0, -1, allow_small_or_imprecise_dtypes=True).then_inc(s.i_t, 1)
             sent = 0
-
-            def send(ap, to, sem):
+            for sem, val, ap, to, rsem in ((s.i_t, 1, table, home, s["t%d" % i]),
+                                           (s["l%d" % r], here, T.lend[:, _lslot(r)], dst, s["l%d" % r]),
+                                           (s["x%d" % r], here, T.win[:, _xslot(r)], dst, s["x%d" % r])):
                 rid, pid, _ = topo.addr(to)
                 em = m & topo.mask(core, to)
-                g.remote_dma(out_ap=ap, in_ap=ap, remote_sem=sem, local_sem=s.ls, pid=pid, routing_id=rid,
+                g.wait_ge(sem, val)
+                g.remote_dma(out_ap=ap, in_ap=ap, remote_sem=rsem, local_sem=s.ls, pid=pid, routing_id=rid,
                              dma_engine_mask=em)
-                return _engines(em)
-
-            g.iota(T.diff[:], [[1, 128]], 0, -1, allow_small_or_imprecise_dtypes=True).then_inc(s.i_d, 1)
-            if i == 0:
-                g.wait_ge(s.i_d, 1)
-                sent += send(T.diff[:], home, s.t0)
-            else:
-                g.iota(T.val[:], [[0, 8], [1, 16]], 0, -1, allow_small_or_imprecise_dtypes=True).then_inc(s.i_t, 1)
-                g.wait_ge(s.i_t, 1)
-                sent += send(T.val[:], home, s.t1)
-            v.wait_ge(s.i_d, 1)
-            v.tensor_scalar(T.tri[:], T.diff[:], 0.0, None, Op.is_gt).then_inc(s.c_tri, 1)
-            lens = T.lend[:, LW * r + 1:LW * r + 17]
-            v.wait_ge(s["l%d" % r], here)
-            v.transpose(T.ltr[:], T.lraw[:]).then_inc(s.tr, 1)
-            v.wait_ge(s.tr, 1)
-            v.tensor_scalar(lens, T.ltr[:, 16:32], 2.0, None, Op.mult).then_inc(s.lo, 1)
-            pe.wait_ge(s.c_tri, 1)
-            pe.wait_ge(s.lo, 1)
-            pe.matmul(T.psb[:, 0:16], T.tri[:], lens, True, True).then_inc(s.pb, 1)
-            v.wait_ge(s.pb, 1)
-            v.tensor_reduce(T.lend[:, LW * r:LW * r + 1], T.psb[:, 0:16], AxisListType.X, Op.add).then_inc(s.bs, 1)
-            g.wait_ge(s.lo, 1)
-            g.wait_ge(s.bs, 1)
-            sent += send(T.lend[:, _lslot(r)], dst, s["l%d" % r])
-            g.wait_ge(s["x%d" % r], here)
-            sent += send(T.win[:, _xslot(r)], dst, s["x%d" % r])
+                sent += _engines(em)
             g.wait_ge(s.ls, sent)
 
 
@@ -152,60 +132,63 @@ def _rank(g, core, r, T, topo):
                 inc[o] = _engines(topo.mask(relay, core))
 
     sy.dma_start(T.lnat[32 * r + 16:32 * r + 32, :], T.ln[:]).then_inc(s.dl, 16)
-    sc.dma_start(T.win[:, _xslot(r)], T.x[:]).then_inc(s.dx, 16)
+    sy.dma_start(T.win[:, _xslot(r)], T.x[:]).then_inc(s.dx, 16)
 
-    if r < min(near):
-        table = T.thr[:, 0:NC + 1]
-        g.iota(table, [[2 * QB, NC + 1]], -QB, 0, allow_small_or_imprecise_dtypes=True).then_inc(s.i_t, 1)
-    else:
-        table = T.qtab[:]
-        g.iota(table, [[2, QB]], 1 - QB, 0, allow_small_or_imprecise_dtypes=True).then_inc(s.i_t, 1)
+    h0 = QB // 2 if r > min(near) else 0
+    table = T.qtab[:, h0:h0 + QB // 2]
+    g.iota(table, [[2, QB // 2]], 2 * h0 + 1 - QB, 0, allow_small_or_imprecise_dtypes=True).then_inc(s.i_t, 1)
     sent = 0
 
-    def send(src, out, sem, cores):
+    def send(ap, sem, cores):
         m = topo.mask(core, cores[0])
         g.remote_dma_fused([RemoteDMATransfer(dst_ids=[_dst(topo, c) for c in cores], dma_engine_mask=m, remote_sem=sem,
-                                              srcs=[src], dsts=[out for _ in cores])], local_sem=s.ls)
+                                              srcs=[ap], dsts=[ap for _ in cores])], local_sem=s.ls)
         return _engines(m)
 
     hop = [c for c, _ in relays]
     nb = [T.cores[o] for o in near]
     own = T.win[:, _xslot(r)]
     g.wait_ge(s.i_t, 1)
-    sent += send(table, table, s.tn, nb)
-    g.wait_ge(s.mz, 4)
-    g.wait_ge(s.dl, 16)
-    sent += send(T.lnat[:], T.lraw[:], s["l%d" % r], hop)
-    sent += send(T.lnat[:], T.lraw[:], s["l%d" % r], nb)
+    sent += send(table, s.tn, nb)
+    g.wait_ge(s.me, 1)
+    g.wait_ge(s.lo, 1)
+    g.wait_ge(s.bs, 1)
+    sent += send(T.lend[:, _lslot(r)], s["l%d" % r], hop + nb)
     g.wait_ge(s.dx, 16)
-    sent += send(own, own, s["x%d" % r], hop)
-    sent += send(own, own, s["x%d" % r], nb)
+    sent += send(own, s["x%d" % r], hop)
+    sent += send(own, s["x%d" % r], nb)
 
-    for b in range(4):
-        v.memset(T.lnat[32 * b:32 * b + (16 if b == r else 32), :], 0).then_inc(s.mz, 1)
-    v.memset(T.win[:, 4 * J:4 * J + 8], 0.0).then_inc(s.mw, 1)
+    mine = slice(32 * r, 32 * r + 32)
+    lown = T.lend[mine, LW * r + 1:LW * r + 17]
+    v.memset(T.ones[mine, :], 1.0).then_inc(s.mo, 1)
+    v.memset(T.lnat[32 * r:32 * r + 16, :], 0).then_inc(s.mz, 1)
+    v.wait_ge(s.mo, 1)
+    v.tensor_tensor_scan(T.idx[mine, :], T.ones[mine, :], T.ones[mine, :], 0.0, Op.add, Op.mult).then_inc(s.c_ix, 1)
+    v.memset(T.lend[:, _lslot(r)], 0.0).then_inc(s.me, 1)
+    nt = 1
+    if r > 0:
+        v.memset(T.tri[mine, 0:32 * r], 0.0).then_inc(s.mt, 1)
+    if r < 3:
+        v.memset(T.tri[mine, 32 * r + 32:128], 1.0).then_inc(s.mt, 1)
+    nt = int(r > 0) + int(r < 3)
+    v.wait_ge(s.c_ix, 1)
+    v.transpose(T.idxt[mine, :], T.idx[mine, :]).then_inc(s.c_it, 1)
     v.memset(T.shift[:, 0:1], float(1 - QB - 2 * Q * r)).then_inc(s.ms, 1)
-    v.memset(T.shift[:, 1:16], 0.0).then_inc(s.ms, 1)
-
-    v.wait_ge(s.mz, 4)
+    v.wait_ge(s.c_it, 1)
+    v.tensor_tensor(T.tri[mine, mine], T.idx[mine, :], T.idxt[mine, :], Op.is_gt).then_inc(s.c_tri, 1)
+    v.wait_ge(s.mz, 1)
+    v.wait_ge(s.me, 1)
     v.wait_ge(s.dl, 16)
-    v.wait_ge(s["l%d" % near[0]], inc[near[0]])
-    v.tensor_tensor(T.lsum[:], T.lnat[:], T.lraw[:], Op.add).then_inc(s.su, 1)
-    v.wait_ge(s.t0, tinc[0])
-    v.tensor_scalar(T.tri[:], T.diff[:], 0.0, None, Op.is_gt).then_inc(s.c_tri, 1)
-    v.wait_ge(s.su, 1)
-    v.transpose(T.ltr[:], T.lsum[:]).then_inc(s.tr, 1)
+    v.transpose(T.ltr[mine, :], T.lnat[mine, :]).then_inc(s.tr, 1)
     v.wait_ge(s.tr, 1)
-    v.tensor_scalar(T.lchip[:], T.ltr[:, 16:32], 2.0, None, Op.mult).then_inc(s.lo, 1)
+    v.tensor_scalar(lown, T.ltr[mine, 16:32], 2.0, None, Op.mult).then_inc(s.lo, 1)
+    pe.wait_ge(s.mt, nt)
     pe.wait_ge(s.c_tri, 1)
     pe.wait_ge(s.lo, 1)
-    pe.matmul(T.psb[:, 0:16], T.tri[:], T.lchip[:], True, True).then_inc(s.pb, 1)
-    v.wait_ge(s.lo, 1)
-    v.wait_ge(s.ms, 2)
+    pe.matmul(T.psb[:, 0:16], T.tri[mine, :], lown, True, True).then_inc(s.pb, 1)
+    v.memset(T.win[:, 4 * J:4 * J + 8], 0.0).then_inc(s.mw, 1)
     v.wait_ge(s.pb, 1)
-    v.tensor_reduce(T.base[:, 0:1], T.psb[:, 0:16], AxisListType.X, Op.add).then_inc(s.bs, 1)
-    v.wait_ge(s.bs, 1)
-    v.tensor_tensor_scan(T.echip[:], T.lchip[:], T.shift[:], T.base[:, 0:1], Op.add, Op.add).then_inc(s.ec, 1)
+    v.tensor_reduce(T.lend[:, LW * r:LW * r + 1], T.psb[:, 0:16], AxisListType.X, Op.add).then_inc(s.bs, 1)
 
     v.wait_ge(s.t1, tinc[1])
     v.tensor_scalar(T.pcol[:, 0:1], T.val[0:32, 0:1], float(1 - QB), -0.5, Op.is_equal, Op.mult).then_inc(s.c_pc, 1)
@@ -216,18 +199,27 @@ def _rank(g, core, r, T, topo):
     for h in range(2):
         v.tensor_scalar(T["dn%d" % h][:], T["up%d" % h][:], -1.0, T.pcol[:, 0:1], Op.mult, Op.add).then_inc(s.c_dn, 1)
 
+    n0, n1 = LW * r, LW * near[0]
+    v.wait_ge(s.lo, 1)
+    v.wait_ge(s.bs, 1)
+    v.wait_ge(s.ms, 1)
+    v.wait_ge(s["l%d" % near[0]], inc[near[0]])
+    v.tensor_tensor_scan(T.echip[:, 0:17], T.lend[:, n0:n0 + 17], T.lend[:, n1:n1 + 17], T.shift[:, 0:1],
+                         Op.add, Op.add).then_inc(s.ec, 1)
+
     v.wait_ge(s.ec, 1)
+    v.wait_ge(s.i_t, 1)
+    v.wait_ge(s.tn, inc[near[0]])
     for q in (v, sc):
-        q.wait_ge(s.i_t, 1)
-        q.wait_ge(s.tn, inc[near[0]])
+        q.wait_ge(s.t0, tinc[0])
     for o in far:
         v.wait_ge(s["l%d" % o], inc[o])
     there = slice(32 * min(far), 32 * max(far) + 32)
     here = slice(32 * min(near + [r]), 32 * max(near + [r]) + 32)
     f0, f1 = LW * far[0], LW * far[1]
-    v.tensor_tensor_scan(T.ends[there, 0:17], T.lend[there, f0:f0 + 17], T.lend[there, f1:f1 + 17], T.echip[there, 0:1],
+    v.tensor_tensor_scan(T.ends[there, 0:17], T.lend[there, f0:f0 + 17], T.lend[there, f1:f1 + 17], T.echip[there, 16:17],
                          Op.add, Op.add).then_inc(s.en, 1)
-    v.tensor_scalar(T.ends[here, 1:17], T.echip[here, :], T.lend[here, f0:f0 + 1], T.lend[here, f1:f1 + 1],
+    v.tensor_scalar(T.ends[here, 1:17], T.echip[here, 1:17], T.lend[here, f0:f0 + 1], T.lend[here, f1:f1 + 1],
                     Op.add, Op.add).then_inc(s.en, 1)
     group = [i for i, (t0, t1) in enumerate(GROUPS) for _ in range(t0, t1)]
     thr = T.thr[:, 0:NC + 1]

@@ -10,7 +10,7 @@ NV = 1
 ROUND = 1.5 * 2.0 ** 29
 GROUPS = ((0, 6), (6, 11), (11, 14), (14, 16))
 LW = 20
-STEPS = (256, 320, 256, 192)
+STEPS = (352, 384, 288)
 
 SCRATCH = {
     "win": ("sbuf", [128, 4 * J + 8], "bfloat16"),
@@ -134,7 +134,8 @@ def _rank(g, core, r, T, topo):
     sy.dma_start(T.lnat[32 * r + 16:32 * r + 32, :], T.ln[:]).then_inc(s.dl, 16)
     sy.dma_start(T.win[:, _xslot(r)], T.x[:]).then_inc(s.dx, 16)
 
-    h0 = QB // 2 if r > min(near) else 0
+    second = int(r > min(near))
+    h0 = QB // 2 * second
     table = T.qtab[:, h0:h0 + QB // 2]
     g.iota(table, [[2, QB // 2]], 2 * h0 + 1 - QB, 0, allow_small_or_imprecise_dtypes=True).then_inc(s.i_t, 1)
     sent = 0
@@ -148,44 +149,46 @@ def _rank(g, core, r, T, topo):
     hop = [c for c, _ in relays]
     nb = [T.cores[o] for o in near]
     own = T.win[:, _xslot(r)]
+    mine = T.lend[:, _lslot(r)]
     g.wait_ge(s.i_t, 1)
     sent += send(table, s.tn, nb)
     g.wait_ge(s.me, 1)
     g.wait_ge(s.lo, 1)
     g.wait_ge(s.bs, 1)
-    sent += send(T.lend[:, _lslot(r)], s["l%d" % r], hop + nb)
+    sent += send(mine, s["l%d" % r], hop)
+    sent += send(mine, s["l%d" % r], nb)
     g.wait_ge(s.dx, 16)
-    sent += send(own, s["x%d" % r], hop)
+    for i in range(len(hop)):
+        sent += send(own, s["x%d" % r], [hop[(i + second) % len(hop)]])
     sent += send(own, s["x%d" % r], nb)
 
-    mine = slice(32 * r, 32 * r + 32)
-    lown = T.lend[mine, LW * r + 1:LW * r + 17]
-    v.memset(T.ones[mine, :], 1.0).then_inc(s.mo, 1)
+    block = slice(32 * r, 32 * r + 32)
+    lown = T.lend[block, LW * r + 1:LW * r + 17]
+    v.memset(T.ones[block, :], 1.0).then_inc(s.mo, 1)
     v.memset(T.lnat[32 * r:32 * r + 16, :], 0).then_inc(s.mz, 1)
     v.wait_ge(s.mo, 1)
-    v.tensor_tensor_scan(T.idx[mine, :], T.ones[mine, :], T.ones[mine, :], 0.0, Op.add, Op.mult).then_inc(s.c_ix, 1)
-    v.memset(T.lend[:, _lslot(r)], 0.0).then_inc(s.me, 1)
-    nt = 1
-    if r > 0:
-        v.memset(T.tri[mine, 0:32 * r], 0.0).then_inc(s.mt, 1)
-    if r < 3:
-        v.memset(T.tri[mine, 32 * r + 32:128], 1.0).then_inc(s.mt, 1)
-    nt = int(r > 0) + int(r < 3)
+    v.tensor_tensor_scan(T.idx[block, :], T.ones[block, :], T.ones[block, :], 0.0, Op.add, Op.mult).then_inc(s.c_ix, 1)
+    v.memset(mine, 0.0).then_inc(s.me, 1)
+    fills = 0
+    for a, b, c in ((0, 32 * r, 0.0), (32 * r + 32, 128, 1.0)):
+        if b > a:
+            v.memset(T.tri[block, a:b], c).then_inc(s.mt, 1)
+            fills += 1
     v.wait_ge(s.c_ix, 1)
-    v.transpose(T.idxt[mine, :], T.idx[mine, :]).then_inc(s.c_it, 1)
+    v.transpose(T.idxt[block, :], T.idx[block, :]).then_inc(s.c_it, 1)
     v.memset(T.shift[:, 0:1], float(1 - QB - 2 * Q * r)).then_inc(s.ms, 1)
     v.wait_ge(s.c_it, 1)
-    v.tensor_tensor(T.tri[mine, mine], T.idx[mine, :], T.idxt[mine, :], Op.is_gt).then_inc(s.c_tri, 1)
+    v.tensor_tensor(T.tri[block, block], T.idx[block, :], T.idxt[block, :], Op.is_gt).then_inc(s.c_tri, 1)
     v.wait_ge(s.mz, 1)
     v.wait_ge(s.me, 1)
     v.wait_ge(s.dl, 16)
-    v.transpose(T.ltr[mine, :], T.lnat[mine, :]).then_inc(s.tr, 1)
+    v.transpose(T.ltr[block, :], T.lnat[block, :]).then_inc(s.tr, 1)
     v.wait_ge(s.tr, 1)
-    v.tensor_scalar(lown, T.ltr[mine, 16:32], 2.0, None, Op.mult).then_inc(s.lo, 1)
-    pe.wait_ge(s.mt, nt)
+    v.tensor_scalar(lown, T.ltr[block, 16:32], 2.0, None, Op.mult).then_inc(s.lo, 1)
+    pe.wait_ge(s.mt, fills)
     pe.wait_ge(s.c_tri, 1)
     pe.wait_ge(s.lo, 1)
-    pe.matmul(T.psb[:, 0:16], T.tri[mine, :], lown, True, True).then_inc(s.pb, 1)
+    pe.matmul(T.psb[:, 0:16], T.tri[block, :], lown, True, True).then_inc(s.pb, 1)
     v.memset(T.win[:, 4 * J:4 * J + 8], 0.0).then_inc(s.mw, 1)
     v.wait_ge(s.pb, 1)
     v.tensor_reduce(T.lend[:, LW * r:LW * r + 1], T.psb[:, 0:16], AxisListType.X, Op.add).then_inc(s.bs, 1)

from concourse.bass import DstId, RemoteDMATransfer
from concourse.mybir import AluOpType as Op, AxisListType, ActivationFunctionType as Act

J, Q = 512, 2048
NT = 16
QB = 32
NC = Q // QB
SW = 72
NV = 1
ROUND = 1.5 * 2.0 ** 29
GROUPS = ((0, 6), (6, 11), (11, 14), (14, 16))
LW = 20
STEPS = (352, 384, 288)

SCRATCH = {
    "win": ("sbuf", [128, 4 * J + 8], "bfloat16"),
    "lnat": ("sbuf", [128, 32], "int32"),
    "ltr": ("sbuf", [128, 32], "int32"),
    "lend": ("sbuf", [128, 4 * LW], "float32"),
    "shift": ("sbuf", [128, 4], "float32"),
    "echip": ("sbuf", [128, LW], "float32"),
    "ends": ("sbuf", [128, LW], "float32"),
    "zblk": ("sbuf", [128, 16], "float32"),
    "ones": ("sbuf", [128, 32], "float32"),
    "idx": ("sbuf", [128, 32], "float32"),
    "idxt": ("sbuf", [128, 32], "float32"),
    "tri": ("sbuf", [128, 128], "float32"),
    "val": ("sbuf", [128, 128], "bfloat16"),
    "thr": ("sbuf", [128, SW], "bfloat16"),
    "qtab": ("sbuf", [128, QB], "bfloat16"),
    "pcol": ("sbuf", [32, 4], "float32"),
    "up0": ("sbuf", [32, 128], "float16"),
    "up1": ("sbuf", [32, 128], "float16"),
    "dn0": ("sbuf", [32, 128], "float16"),
    "dn1": ("sbuf", [32, 128], "float16"),
    "ah": ("sbuf", [128, NT * QB], "bfloat16"),
    "sg": ("sbuf", [128, NT * SW], "bfloat16"),
    "wh": ("sbuf", [32, SW], "float16"),
    "off": ("sbuf", [128, 128], "uint16"),
    "yo": ("sbuf", [128, Q], "bfloat16"),
    "psb": ("psum", [128, 512], "float32"),
    "psw": ("psum", [128, 512], "float32"),
    "pso0": ("psum", [128, 512], "float32"),
    "pso1": ("psum", [128, 512], "float32"),
}
SEMAPHORES = (["l0", "l1", "l2", "l3", "x0", "x1", "x2", "x3", "t0", "t1", "tn", "ls", "dl", "dx", "st"]
              + ["mz", "me", "mo", "mt", "mw", "ms", "tr", "i_t", "c_ix", "c_it", "c_tri", "c_pc", "c_up", "c_dn", "lo", "pb",
                 "bs", "ec", "en", "em", "pw", "wc", "po0", "po1", "of"]
              + ["a%d" % i for i in range(len(GROUPS))] + ["s%d" % i for i in range(len(GROUPS))]
              + ["yv%d" % i for i in range(len(STEPS))] + ["ys%d" % i for i in range(len(STEPS))])


def _engines(mask):
    return bin(mask).count("1")


def _routes(T, topo, rank):
    me = T.cores[rank]
    near = [r for r, c in enumerate(T.cores) if c != me and topo.chip(c) == topo.chip(me)]
    far = [r for r, c in enumerate(T.cores) if topo.chip(c) != topo.chip(me)]
    hi = me
    while topo.chip(hi + 1) == topo.chip(me):
        hi += 1
    lo = me
    while lo > 0 and topo.chip(lo - 1) == topo.chip(me):
        lo -= 1
    own = [c for c in range(lo, hi + 1) if T.rank_of(c) is None and topo.die(c) == topo.die(me)
           and all(topo.may_write(c, T.cores[f]) for f in far)]
    return near, [(own[i % len(own)], f) for i, f in enumerate(far)]


def _dst(topo, c):
    rid, pid, _ = topo.addr(c)
    return DstId(rid=rid, pnc=pid)


def _lslot(r):
    return slice(LW * r, LW * r + 17)


def _xslot(r):
    return slice(J * r, J * r + J)


def rank_program(g, core, T, topo):
    rank = T.rank_of(core)
    if rank is None:
        _relay(g, core, T, topo)
    else:
        _rank(g, core, rank, T, topo)


def _relay(g, core, T, topo):
    s = T.sem
    for r in range(len(T.cores)):
        for i, (relay, f) in enumerate(_routes(T, topo, r)[1]):
            if relay != core:
                continue
            home, dst = T.cores[r], T.cores[f]
            here = _engines(topo.mask(home, core))
            m = topo.mask(core, dst)
            if i == 0:
                table = T.thr[:, 0:NC + 1]
                g.iota(table, [[2 * QB, NC + 1]], -QB, 0, allow_small_or_imprecise_dtypes=True).then_inc(s.i_t, 1)
            else:
                table = T.val[:]
                g.iota(table, [[0, 8], [1, 16]], 0, -1, allow_small_or_imprecise_dtypes=True).then_inc(s.i_t, 1)
            sent = 0
            for sem, val, ap, to, rsem in ((s.i_t, 1, table, home, s["t%d" % i]),
                                           (s["l%d" % r], here, T.lend[:, _lslot(r)], dst, s["l%d" % r]),
                                           (s["x%d" % r], here, T.win[:, _xslot(r)], dst, s["x%d" % r])):
                rid, pid, _ = topo.addr(to)
                em = m & topo.mask(core, to)
                g.wait_ge(sem, val)
                g.remote_dma(out_ap=ap, in_ap=ap, remote_sem=rsem, local_sem=s.ls, pid=pid, routing_id=rid,
                             dma_engine_mask=em)
                sent += _engines(em)
            g.wait_ge(s.ls, sent)


def _rank(g, core, r, T, topo):
    s, v, pe, sc, sy = T.sem, g.vector, g.tensor, g.scalar, g.sync
    near, relays = _routes(T, topo, r)
    far = [f for _, f in relays]
    tinc = [_engines(topo.mask(relay, core) & topo.mask(relay, T.cores[f])) for relay, f in relays]
    inc = {}
    for o in near:
        inc[o] = _engines(topo.mask(T.cores[o], core))
    for o in far:
        for relay, f in _routes(T, topo, o)[1]:
            if f == r:
                inc[o] = _engines(topo.mask(relay, core))

    sy.dma_start(T.lnat[32 * r + 16:32 * r + 32, :], T.ln[:]).then_inc(s.dl, 16)
    sy.dma_start(T.win[:, _xslot(r)], T.x[:]).then_inc(s.dx, 16)

    second = int(r > min(near))
    h0 = QB // 2 * second
    table = T.qtab[:, h0:h0 + QB // 2]
    g.iota(table, [[2, QB // 2]], 2 * h0 + 1 - QB, 0, allow_small_or_imprecise_dtypes=True).then_inc(s.i_t, 1)
    sent = 0

    def send(ap, sem, cores):
        m = topo.mask(core, cores[0])
        g.remote_dma_fused([RemoteDMATransfer(dst_ids=[_dst(topo, c) for c in cores], dma_engine_mask=m, remote_sem=sem,
                                              srcs=[ap], dsts=[ap for _ in cores])], local_sem=s.ls)
        return _engines(m)

    hop = [c for c, _ in relays]
    nb = [T.cores[o] for o in near]
    own = T.win[:, _xslot(r)]
    mine = T.lend[:, _lslot(r)]
    g.wait_ge(s.i_t, 1)
    sent += send(table, s.tn, nb)
    g.wait_ge(s.me, 1)
    g.wait_ge(s.lo, 1)
    g.wait_ge(s.bs, 1)
    sent += send(mine, s["l%d" % r], hop)
    sent += send(mine, s["l%d" % r], nb)
    g.wait_ge(s.dx, 16)
    for i in range(len(hop)):
        sent += send(own, s["x%d" % r], [hop[(i + second) % len(hop)]])
    sent += send(own, s["x%d" % r], nb)

    block = slice(32 * r, 32 * r + 32)
    lown = T.lend[block, LW * r + 1:LW * r + 17]
    v.memset(T.ones[block, :], 1.0).then_inc(s.mo, 1)
    v.memset(T.lnat[32 * r:32 * r + 16, :], 0).then_inc(s.mz, 1)
    v.wait_ge(s.mo, 1)
    v.tensor_tensor_scan(T.idx[block, :], T.ones[block, :], T.ones[block, :], 0.0, Op.add, Op.mult).then_inc(s.c_ix, 1)
    v.memset(mine, 0.0).then_inc(s.me, 1)
    fills = 0
    for a, b, c in ((0, 32 * r, 0.0), (32 * r + 32, 128, 1.0)):
        if b > a:
            v.memset(T.tri[block, a:b], c).then_inc(s.mt, 1)
            fills += 1
    v.wait_ge(s.c_ix, 1)
    v.transpose(T.idxt[block, :], T.idx[block, :]).then_inc(s.c_it, 1)
    v.memset(T.shift[:, 0:1], float(1 - QB - 2 * Q * r)).then_inc(s.ms, 1)
    v.wait_ge(s.c_it, 1)
    v.tensor_tensor(T.tri[block, block], T.idx[block, :], T.idxt[block, :], Op.is_gt).then_inc(s.c_tri, 1)
    v.wait_ge(s.mz, 1)
    v.wait_ge(s.me, 1)
    v.wait_ge(s.dl, 16)
    v.transpose(T.ltr[block, :], T.lnat[block, :]).then_inc(s.tr, 1)
    v.wait_ge(s.tr, 1)
    v.tensor_scalar(lown, T.ltr[block, 16:32], 2.0, None, Op.mult).then_inc(s.lo, 1)
    pe.wait_ge(s.mt, fills)
    pe.wait_ge(s.c_tri, 1)
    pe.wait_ge(s.lo, 1)
    pe.matmul(T.psb[:, 0:16], T.tri[block, :], lown, True, True).then_inc(s.pb, 1)
    v.memset(T.win[:, 4 * J:4 * J + 8], 0.0).then_inc(s.mw, 1)
    v.wait_ge(s.pb, 1)
    v.tensor_reduce(T.lend[:, LW * r:LW * r + 1], T.psb[:, 0:16], AxisListType.X, Op.add).then_inc(s.bs, 1)

    v.wait_ge(s.t1, tinc[1])
    v.tensor_scalar(T.pcol[:, 0:1], T.val[0:32, 0:1], float(1 - QB), -0.5, Op.is_equal, Op.mult).then_inc(s.c_pc, 1)
    for h in range(2):
        v.tensor_scalar(T["up%d" % h][:], T.val[0:32, :], -16.0 * h, -0.5, Op.is_equal, Op.mult).then_inc(s.c_up, 1)
    v.wait_ge(s.c_pc, 1)
    v.wait_ge(s.c_up, 2)
    for h in range(2):
        v.tensor_scalar(T["dn%d" % h][:], T["up%d" % h][:], -1.0, T.pcol[:, 0:1], Op.mult, Op.add).then_inc(s.c_dn, 1)

    n0, n1 = LW * r, LW * near[0]
    v.wait_ge(s.lo, 1)
    v.wait_ge(s.bs, 1)
    v.wait_ge(s.ms, 1)
    v.wait_ge(s["l%d" % near[0]], inc[near[0]])
    v.tensor_tensor_scan(T.echip[:, 0:17], T.lend[:, n0:n0 + 17], T.lend[:, n1:n1 + 17], T.shift[:, 0:1],
                         Op.add, Op.add).then_inc(s.ec, 1)

    v.wait_ge(s.ec, 1)
    v.wait_ge(s.i_t, 1)
    v.wait_ge(s.tn, inc[near[0]])
    for q in (v, sc):
        q.wait_ge(s.t0, tinc[0])
    for o in far:
        v.wait_ge(s["l%d" % o], inc[o])
    there = slice(32 * min(far), 32 * max(far) + 32)
    here = slice(32 * min(near + [r]), 32 * max(near + [r]) + 32)
    f0, f1 = LW * far[0], LW * far[1]
    v.tensor_tensor_scan(T.ends[there, 0:17], T.lend[there, f0:f0 + 17], T.lend[there, f1:f1 + 17], T.echip[there, 16:17],
                         Op.add, Op.add).then_inc(s.en, 1)
    v.tensor_scalar(T.ends[here, 1:17], T.echip[here, 1:17], T.lend[here, f0:f0 + 1], T.lend[here, f1:f1 + 1],
                    Op.add, Op.add).then_inc(s.en, 1)
    group = [i for i, (t0, t1) in enumerate(GROUPS) for _ in range(t0, t1)]
    thr = T.thr[:, 0:NC + 1]

    def row(t):
        return T.sg[:, SW * t:SW * t + NC + 1]

    def end(t):
        return T.ends[:, t + 1:t + 2]

    sc.wait_ge(s.en, 2)
    for t in range(NV, NT):
        sc.activation(row(t), thr, Act.Sign, bias=end(t), scale=-1.0).then_inc(s["s%d" % group[t]], 1)
    v.wait_ge(s.en, 2)
    v.tensor_scalar(T.zblk[:], T.ends[:, 1:17], ROUND, -ROUND, Op.add, Op.add).then_inc(s.em, 1)
    for t in range(NV):
        v.tensor_scalar(row(t), thr, end(t), 2.0, Op.is_lt, Op.mult).then_inc(s["s%d" % group[t]], 1)
    v.wait_ge(s.em, 1)
    for t in range(NT):
        v.tensor_scalar(T.ah[:, QB * t:QB * t + QB], T.qtab[:], T.zblk[:, t:t + 1], end(t),
                        Op.add, Op.is_ge).then_inc(s["a%d" % group[t]], 1)
    for i, (t0, t1) in enumerate(GROUPS):
        pe.wait_ge(s["a%d" % i], t1 - t0)
        pe.wait_ge(s["s%d" % i], t1 - t0)
        for t in range(t0, t1):
            mm = pe.matmul(T.psw[0:QB, 0:NC + 1], T.ah[:, QB * t:QB * t + QB], row(t), t == 0, t == NT - 1)
    mm.then_inc(s.pw, 1)
    v.wait_ge(s.pw, 1)
    v.tensor_scalar(T.wh[:, 0:NC + 1], T.psw[0:QB, 0:NC + 1], -128.0 * NV, None, Op.add).then_inc(s.wc, 1)
    pe.wait_ge(s.c_up, 2)
    pe.wait_ge(s.c_dn, 2)
    pe.wait_ge(s.wc, 1)
    for h in range(2):
        out = T["pso%d" % h][:, 0:NC]
        pe.matmul(out, T["up%d" % h][:], T.wh[:, 1:NC + 1], True, False)
        pe.matmul(out, T["dn%d" % h][:], T.wh[:, 0:NC], False, True).then_inc(s["po%d" % h], 1)
    for h in range(2):
        v.wait_ge(s["po%d" % h], 1)
        v.tensor_scalar(T.off[:, h::2], T["pso%d" % h][:, 0:NC], float(Q // 2), None, Op.add).then_inc(s.of, 1)

    for q in (v, sc):
        q.wait_ge(s.mw, 1)
        q.wait_ge(s.of, 2)
        q.wait_ge(s.dx, 16)
        for o in near + far:
            q.wait_ge(s["x%d" % o], inc[o])
    win = T.win[:, 0:4 * J + 8]
    at = 0
    for i, w in enumerate(STEPS):
        mid, stop = at + w, at + 2 * w
        v.tensor_copy(T.yo[:, at:mid], win.indirect(T.off[:, at // 16:mid // 16])).then_inc(s["yv%d" % i], 1)
        sc.activation(T.yo[:, mid:stop], win.indirect(T.off[:, mid // 16:stop // 16]), Act.Copy).then_inc(s["ys%d" % i], 1)
        sy.wait_ge(s["yv%d" % i], 1)
        sy.wait_ge(s["ys%d" % i], 1)
        sy.dma_start(T.y[:, at:stop], T.yo[:, at:stop]).then_inc(s.st, 16)
        at = stop
    sy.wait_ge(s.st, 16 * len(STEPS))
    g.wait_ge(s.ls, sent)
